import numpy as np
import ml_dtypes


def mxq(x, axis, fmt="e4m3"):
    dtype, down = {"e4m3": (ml_dtypes.float8_e4m3fn, 7), "e5m2": (ml_dtypes.float8_e5m2, 14)}[fmt]
    v = np.moveaxis(np.asarray(x, np.float32).astype(ml_dtypes.bfloat16).astype(np.float64), axis, -1)
    blocks = v.reshape(v.shape[:-1] + (-1, 32))
    amax = np.abs(blocks).max(-1, keepdims=True)
    byte = np.maximum(np.where(amax > 0, np.frexp(amax)[1] - 1 + 127, 0) - down, 1)
    scale = np.exp2(byte - 127.0)
    codes = (blocks / scale).astype(np.float32).astype(dtype).astype(np.float64)
    return np.moveaxis((codes * scale).reshape(v.shape), -1, axis)


WIDE = False


def mx_kscale(k):
    if not WIDE:
        return np.ones(k)
    levels = np.array([10, -10, 5, -5, 0])
    if k % 512:
        return np.exp2(np.random.permutation(np.resize(levels, k // 32))).repeat(32)
    a = np.empty((k // 512, 16))
    for p in range(k // 512):
        a[p, :8] = np.random.permutation(np.resize(levels, 8))
        for g in range(8):
            far = levels[np.abs(levels - a[p, g]) >= 10]
            a[p, g + 8] = far[np.random.randint(len(far))]
    return np.exp2(a.ravel()).repeat(32)


BF16 = ml_dtypes.bfloat16


def bf(x):
    return np.asarray(x, np.float32).astype(BF16)


def f64(x):
    return np.asarray(x).astype(np.float64)


P, R, H, C = 2048, 512, 256, 1024


def gelu(x):
    return 0.5 * x * (1.0 + np.tanh(np.sqrt(2.0 / np.pi) * (x + 0.044715 * x * x * x)))


def setup_inputs():
    s, t, u = mx_kscale(R), mx_kscale(C), mx_kscale(P)
    x = (np.arange(P) + np.random.random(P)) / P
    phase = 2.0 * np.pi * x[:, None] * (1.0 + np.arange(H))
    basis = np.concatenate([np.cos(phase), np.sin(phase)], axis=1)
    return {"synth": bf(basis * np.sqrt(2.0 / R) * s),
            "coef": bf(np.random.standard_normal((R, C)) / s[:, None]),
            "skip": bf(np.random.standard_normal((P, C))),
            "bias": bf(0.4 * np.random.standard_normal(C)),
            "gain": bf((1.0 + 0.1 * np.random.standard_normal(C)) * t),
            "quad": bf((1.0 + 0.1 * np.random.standard_normal(P)) * u),
            "mix": bf(np.random.standard_normal((C, C)) / np.sqrt(C) / t[:, None]),
            "bias_mix": bf(0.4 * np.random.standard_normal(C)),
            "analysis": bf(basis.T * np.sqrt(2.0 / P) / u),
            "filt_re": bf(np.random.standard_normal((H, C))),
            "filt_im": bf(np.random.standard_normal((H, C)))}


def reference(synth, coef, skip, bias, gain, quad, mix, bias_mix, analysis, filt_re, filt_im):
    z = mxq(f64(synth), 1, "e4m3") @ mxq(f64(coef), 0, "e4m3")
    a = gelu(z + f64(skip) + f64(bias))
    hc = a * f64(gain)
    local = (mxq(hc, 1, "e4m3") @ mxq(f64(mix), 0, "e4m3")) + f64(bias_mix)
    hp = a * f64(quad)[:, None]
    spec = mxq(f64(analysis), 1, "e4m3") @ mxq(hp, 0, "e4m3")
    zc, zs = spec[:H], spec[H:]
    fr, fi = f64(filt_re), f64(filt_im)
    cosine = fr * zc + fi * zs
    sine = fr * zs - fi * zc
    return local, cosine, sine

@@ -1,0 +1,421 @@
+from contextlib import ExitStack
+
+import concourse.mybir as mybir
+from concourse.masks import make_identity
+
+NPTS, NFUN, NMODE, NCH = 2048, 512, 256, 1024
+FLOPS = 2 * (NPTS * NFUN * NCH + NPTS * NCH * NCH + NFUN * NPTS * NCH)
+
+F32 = mybir.dt.float32
+BF16 = mybir.dt.bfloat16
+U32 = mybir.dt.uint32
+U8 = mybir.dt.uint8
+FP8X4 = mybir.dt.float8_e4m3fn_x4
+ACT = mybir.ActivationFunctionType
+ALU = mybir.AluOpType
+
+NCHUNK = 8
+LO_SCALAR = (1, 3, 5, 7)
+LO_STEP = ((), (), (0, 1, 2, 3), (4, 5, 6, 7), (0, 1, 2, 3), (4, 5, 6, 7), (0, 1, 2, 3, 4), (5, 6, 7))
+MIX = (False, True, False, True)
+TAIL = (
+    ("lo", 1, True),
+    ("lo", 2, False),
+    ("spec", 0, 1, ("z", "a"), "gg"),
+    ("lo", 3, True),
+    ("lo", 4, False),
+    ("lo", 5, True),
+    ("spec", 1, 1, ("t", "z"), "vv"),
+    ("lo", 6, False),
+    ("lo", 7, True),
+)
+
+
+def tile_fourier_operator_mix_f6_kernel(
+    tc, synth, coef, skip, bias, gain, quad, mix, bias_mix, analysis, filt_re, filt_im,
+    out_local, out_cos, out_sin,
+):
+    nc = tc.nc
+    with ExitStack() as ctx:
+        ctx.enter_context(nc.allow_non_contiguous_dma("per-channel and per-point vectors"))
+        pool = ctx.enter_context(tc.tile_pool(name="sb", bufs=1))
+        psum = ctx.enter_context(tc.psum_pool(name="ps", bufs=2))
+        ctx.enter_context(tc.manual_schedule())
+
+        def sb(shape, dtype, tag, bufs=1):
+            return pool.tile(shape, dtype, name=tag, tag=tag, bufs=bufs, align_bytes=64)
+
+        def bank(tag):
+            return psum.tile([128, 512], F32, name=tag, tag=tag, bufs=2)
+
+        synth_v = synth.rearrange("(g p j) r -> g p j r", p=128, j=4)
+        coef_v = coef.rearrange("(p j) c -> p j c", j=4)
+        skip_v = skip.rearrange("(g p j) c -> g p j c", p=128, j=4)
+        mix_v = mix.rearrange("(h p j) c -> h p j c", p=128, j=4)
+        an_v = analysis.rearrange("(a b p) k -> a p b k", b=2, p=128)
+        local_v = out_local.rearrange("(g p j) c -> g p j c", p=128, j=4)
+
+        coef_q = sb([128, 2, 512], U32, "coef_q")
+        coef_s = sb([128, 2, 512], U8, "coef_s")
+        syn_q = sb([128, 4, 512], U32, "syn_q")
+        syn_s = sb([128, 4, 512], U8, "syn_s")
+        mix_q = sb([128, 2, 1024], U32, "mix_q")
+        mix_s = sb([128, 2, 1024], U8, "mix_s")
+        an_q = sb([128, 4, 512], U32, "an_q")
+        an_s = sb([128, 4, 512], U8, "an_s")
+        hp_q = sb([128, 4, 1024], U32, "hp_q")
+        hp_s = sb([128, 4, 1024], U8, "hp_s")
+        ident = sb([128, 128], F32, "ident")
+        ones = sb([128, 128], BF16, "ones")
+        brow = sb([128, 1024], BF16, "brow")
+        bias_bc = sb([128, 1024], F32, "bias_bc")
+        rows = sb([128, 512], BF16, "rows")
+        vec = sb([128, 8, 4], F32, "vec")
+        ident_b = sb([128, 128], BF16, "ident_b")
+        warm = sb([128, 1], F32, "warm")
+
+        nc.vector.memset(rows[:], 0.0)
+        nc.vector.memset(ones[:], 1.0)
+        nc.vector.memset(brow[:], 0.0)
+        make_identity(nc, ident[:])
+        nc.vector.tensor_copy(out=ident_b[:], in_=ident[:])
+        nc.scalar.dma_start(out=rows[0:2, :], in_=bias.rearrange("(h k) -> h k", k=512))
+        nc.scalar.dma_start(out=rows[2:4, :], in_=gain.rearrange("(h k) -> h k", k=512))
+        nc.scalar.dma_start(out=rows[4:8, :], in_=quad.rearrange("(g k) -> g k", k=512))
+        nc.scalar.dma_start(out=brow[0:1, :], in_=bias_mix.unsqueeze(0))
+        nc.scalar.activation(out=warm[:], in_=ones[:, 0:1], func=ACT.Gelu_apprx_tanh)
+
+        syn_raw = {}
+        skip_raw = {}
+
+        def load_syn(g):
+            syn_raw[g] = sb([128, 4, 512], BF16, "syn_raw", 2)
+            nc.sync.dma_start(out=syn_raw[g][:], in_=synth_v[g])
+
+        def load_skip(g):
+            skip_raw[g] = sb([128, 4, 1024], BF16, "skip_raw", 2)
+            nc.sync.dma_start(out=skip_raw[g][:], in_=skip_v[g])
+
+        load_syn(0)
+        coef_raw = []
+        coef_raw.append(sb([128, 4, 512], BF16, "r4", 2))
+        nc.sync.dma_start(out=coef_raw[0][:], in_=coef_v[:, :, 0:512])
+        skip_raw[0] = sb([128, 4, 1024], BF16, "skip_raw", 2)
+        nc.sync.dma_start(out=skip_raw[0][:, :, 0:512], in_=skip_v[0][:, :, 0:512])
+        coef_raw.append(sb([128, 4, 512], BF16, "r4", 2))
+        nc.sync.dma_start(out=coef_raw[1][:], in_=coef_v[:, :, 512:1024])
+        nc.sync.dma_start(out=skip_raw[0][:, :, 512:1024], in_=skip_v[0][:, :, 512:1024])
+        load_syn(1)
+        load_skip(1)
+        mix_raw = []
+        for h in range(2):
+            mix_raw.append(sb([128, 4, 1024], BF16, "r8", 2))
+            nc.sync.dma_start(out=mix_raw[h][:], in_=mix_v[h])
+
+        def bias_col(h, t):
+            return vec[:, h, t : t + 1]
+
+        def gain_col(h, t):
+            return vec[:, 2 + h, t : t + 1]
+
+        def quad_cols(g):
+            return vec[:, 4 + g, :]
+
+        def turn_vectors():
+            tb = psum.tile([128, 4, 128], BF16, name="t", tag="t", bufs=2)
+            for t in range(4):
+                nc.tensor.transpose(tb[:, t, :], rows[:, t::4], ident_b[:])
+            nc.vector.tensor_copy(out=vec[:], in_=tb[:, :, 0:8].rearrange("p t r -> p r t"))
+
+        def words_of(t4):
+            return t4[:].rearrange("p c j -> p (c j)").bitcast(F32)
+
+        def turn(src_words, col0, grp):
+            for q in range(2):
+                tb = bank("t")
+                for u in range(2):
+                    for i in range(2):
+                        src = src_words[2 * q + i]
+                        o = (2 * u + i) * 128
+                        nc.tensor.transpose(
+                            tb[:, o : o + 128], src[:, col0 + u : col0 + 256 : 2], ident[:]
+                        )
+                nc.scalar.copy(
+                    out=words_of(grp)[:, 512 * q : 512 * (q + 1)].rearrange("p (r u) -> p r u", u=2),
+                    in_=tb[:].rearrange("p (u r) -> p r u", u=2),
+                )
+
+        def quant(codes, scales, grp):
+            nc.vector.quantize_mx(
+                out=codes.bitcast(FP8X4), scales=scales, in_=grp[:].rearrange("p c j -> p (c j)")
+            )
+
+        def turn_syn(g):
+            grp = sb([128, 512, 4], BF16, "grp", 4)
+            turn([syn_raw[g][:, j, :].bitcast(F32) for j in range(4)], 0, grp)
+            return lambda: quant(syn_q[:, g, :], syn_s[:, g, :], grp)
+
+        def turn_an(k):
+            grp = sb([128, 512, 4], BF16, "grp", 4)
+            turn([an_raw[a][:, b, :].bitcast(F32) for a in range(2) for b in range(2)], 256 * k, grp)
+            return lambda: quant(an_q[:, k, :], an_s[:, k, :], grp)
+
+        sk = {}
+
+        def turn_skip(c):
+            g, h = c // 2, c % 2
+            sk[c] = sb([128, 2, 512, 2], BF16, "sk", 2)
+            skw = sk[c][:].rearrange("p u n e -> p (u n e)").bitcast(F32)
+            for u in range(2):
+                tb = bank("t")
+                for j in range(4):
+                    src = skip_raw[g][:, j, :].bitcast(F32)
+                    nc.tensor.transpose(
+                        tb[:, 128 * j : 128 * (j + 1)],
+                        src[:, 256 * h + u : 256 * (h + 1) : 2],
+                        ident[:],
+                    )
+                nc.scalar.copy(out=skw[:, 512 * u : 512 * (u + 1)], in_=tb[:])
+
+        act_t = {}
+        pair = {}
+
+        def first(c, t):
+            g, h = c // 2, c % 2
+            if t == 0:
+                act_t[c] = sb([128, 4, 512], F32, "act", 2)
+                pair[c] = sb([128, 2, 512, 2], BF16, "pair", 2)
+            zb = bank("z")
+            nc.tensor.matmul_mx(
+                out=zb[:],
+                lhsT=coef_q[:, h, 128 * t : 128 * (t + 1)].bitcast(FP8X4),
+                lhsT_scale=coef_s[:, h, 128 * t : 128 * (t + 1)],
+                rhs=syn_q[:, g, :].bitcast(FP8X4),
+                rhs_scale=syn_s[:, g, :],
+                start=True,
+                stop=True,
+            )
+            x = sb([128, 512], F32, "x", 6)
+            nc.vector.tensor_tensor(
+                out=x[:], in0=zb[:], in1=sk[c][:, t // 2, :, t % 2], op=ALU.add
+            )
+            nc.scalar.activation(
+                out=act_t[c][:, t, :], in_=x[:], func=ACT.Gelu_apprx_tanh, bias=bias_col(h, t)
+            )
+            nc.gpsimd.tensor_scalar(
+                out=pair[c][:, t // 2, :, t % 2],
+                in0=act_t[c][:, t, :],
+                scalar1=gain_col(h, t),
+                scalar2=0.0,
+                op0=ALU.mult,
+                op1=ALU.add,
+            )
+
+        hc_b = {}
+        hc_q = {}
+        hc_s = {}
+
+        def weave_hc(c):
+            hc_b[c] = sb([128, 512, 4], BF16, "hcb", 2)
+            nc.scalar.copy(
+                out=words_of(hc_b[c]).rearrange("p (n u) -> p n u", u=2),
+                in_=pair[c][:].rearrange("p u n e -> p (u n e)").bitcast(F32).rearrange(
+                    "p (u n) -> p n u", u=2
+                ),
+            )
+
+        def quant_hc(c):
+            g, h = c // 2, c % 2
+            if h == 0:
+                hc_q[g] = sb([128, 2, 512], U32, "hc_q", 2)
+                hc_s[g] = sb([128, 2, 512], U8, "hc_s", 2)
+            quant(hc_q[g][:, h, :], hc_s[g][:, h, :], hc_b[c])
+
+        hp_b = {}
+
+        def turn_act(c, t):
+            g = c // 2
+            if t == 0:
+                hp_b[c] = sb([128, 512, 4], BF16, "hpb", 2)
+            tb = bank("a")
+            for j in range(4):
+                nc.tensor.transpose(
+                    tb[:, 128 * j : 128 * (j + 1)],
+                    act_t[c][:, t, 128 * j : 128 * (j + 1)],
+                    ident[:],
+                )
+            nc.vector.tensor_tensor(
+                out=hp_b[c][:, 128 * t : 128 * (t + 1), :],
+                in0=tb[:].rearrange("p (j m) -> p m j", j=4),
+                in1=quad_cols(g).unsqueeze(1).to_broadcast([128, 128, 4]),
+                op=ALU.mult,
+            )
+
+        def quant_hp(c):
+            g, h = c // 2, c % 2
+            cols = slice(512 * h, 512 * (h + 1))
+            quant(hp_q[:, g, cols], hp_s[:, g, cols], hp_b[c])
+
+
+        def local(g, i, on_scalar):
+            nh, j = i // 4, i % 4
+            cols = slice(512 * nh, 512 * (nh + 1))
+            lb = bank("l")
+            for h in range(2):
+                nc.tensor.matmul_mx(
+                    out=lb[:],
+                    lhsT=hc_q[g][:, h, 128 * j : 128 * (j + 1)].bitcast(FP8X4),
+                    lhsT_scale=hc_s[g][:, h, 128 * j : 128 * (j + 1)],
+                    rhs=mix_q[:, h, cols].bitcast(FP8X4),
+                    rhs_scale=mix_s[:, h, cols],
+                    start=(h == 0),
+                    stop=(h == 1),
+                )
+            o = sb([128, 512], F32, "lout", 8)
+            if on_scalar:
+                nc.scalar.copy(out=o[:], in_=lb[:])
+                nc.gpsimd.tensor_tensor(out=o[:], in0=o[:], in1=bias_bc[:, cols], op=ALU.add)
+            else:
+                nc.vector.tensor_tensor(out=o[:], in0=lb[:], in1=bias_bc[:, cols], op=ALU.add)
+            nc.sync.dma_start(out=local_v[g][:, j, cols], in_=o[:])
+
+        coef_g = {}
+
+        def weave_coef(h):
+            coef_g[h] = sb([128, 512, 4], BF16, "grp", 4)
+            nc.vector.tensor_copy(
+                out=coef_g[h][:].rearrange("p (t m) j -> p t m j", t=4),
+                in_=coef_raw[h][:].rearrange("p j (m t) -> p t m j", t=4),
+            )
+
+        def weave_mix(h, nh, on_scalar):
+            grp = sb([128, 512, 4], BF16, "grp", 4)
+            src = mix_raw[h][:, :, 512 * nh : 512 * (nh + 1)].rearrange("p j c -> p c j")
+            if on_scalar:
+                nc.scalar.copy(out=grp[:], in_=src)
+            else:
+                nc.vector.tensor_copy(out=grp[:], in_=src)
+            cols = slice(512 * nh, 512 * (nh + 1))
+            return lambda: quant(mix_q[:, h, cols], mix_s[:, h, cols], grp)
+
+        spec_n = [0]
+
+        def spec(i, h, tags, add_engines):
+            cols = slice(512 * h, 512 * (h + 1))
+            zz = []
+            for part in range(2):
+                mt = 2 * part + i
+                sbk = bank(tags[part])
+                for g in range(4):
+                    nc.tensor.matmul_mx(
+                        out=sbk[:],
+                        lhsT=an_q[:, g, 128 * mt : 128 * (mt + 1)].bitcast(FP8X4),
+                        lhsT_scale=an_s[:, g, 128 * mt : 128 * (mt + 1)],
+                        rhs=hp_q[:, g, cols].bitcast(FP8X4),
+                        rhs_scale=hp_s[:, g, cols],
+                        start=(g == 0),
+                        stop=(g == 3),
+                    )
+                zz.append(sbk[:].rearrange("p (t m) -> p m t", t=4))
+            fr = fre[:, i, cols].rearrange("p (m t) -> p m t", t=4)
+            fi = fim[:, i, cols].rearrange("p (m t) -> p m t", t=4)
+            prods = []
+            for f, z in ((fr, zz[0]), (fi, zz[0]), (fi, zz[1]), (fr, zz[1])):
+                pt = sb([128, 512], F32, "x", 6)
+                nc.vector.tensor_tensor(
+                    out=pt[:].rearrange("p (m t) -> p m t", t=4), in0=z, in1=f, op=ALU.mult
+                )
+                prods.append(pt)
+            for a, b, op, dst, e in (
+                (prods[0], prods[2], ALU.add, out_cos, add_engines[0]),
+                (prods[3], prods[1], ALU.subtract, out_sin, add_engines[1]),
+            ):
+                o = sb([128, 512], F32, "fo", 3)
+                eng = nc.gpsimd if e == "g" else nc.vector
+                eng.tensor_tensor(out=o[:], in0=a[:], in1=b[:], op=op)
+                nc.sync.dma_start(out=dst[128 * i : 128 * (i + 1), cols], in_=o[:])
+
+        q_syn0 = turn_syn(0)
+        load_syn(2)
+        weave_coef(0)
+        q_syn0()
+        quant(coef_q[:, 0, :], coef_s[:, 0, :], coef_g[0])
+        turn_skip(0)
+        turn_vectors()
+        weave_coef(1)
+        first(0, 0)
+        quant(coef_q[:, 1, :], coef_s[:, 1, :], coef_g[1])
+        first(0, 1)
+        turn_skip(1)
+        load_skip(2)
+        first(0, 2)
+        first(0, 3)
+        q_syn1 = turn_syn(1)
+        load_syn(3)
+        pending = [q_syn1]
+
+        for c in range(NCHUNK):
+            los = [((c - 2) // 2, i) for i in LO_STEP[c]]
+            half = (len(los) + 1) // 2
+
+            if c + 1 < NCHUNK:
+                first(c + 1, 0)
+                first(c + 1, 1)
+            for q in pending:
+                q()
+            pending = []
+            for g, i in los[:half]:
+                local(g, i, i in LO_SCALAR)
+            turn_act(c, 0)
+            turn_act(c, 1)
+            if c + 2 < NCHUNK:
+                turn_skip(c + 2)
+                if c == 1:
+                    load_skip(3)
+            weave_hc(c)
+            if c + 1 < NCHUNK:
+                first(c + 1, 2)
+                first(c + 1, 3)
+            for g, i in los[half:]:
+                local(g, i, i in LO_SCALAR)
+            if c == 7:
+                spec(0, 0, ("z", "z"), "gg")
+            quant_hc(c)
+            turn_act(c, 2)
+            turn_act(c, 3)
+            after = []
+            if c == 0:
+                after = [weave_mix(0, 0, MIX[0])]
+                for nh in range(2):
+                    bb = bank("l")
+                    nc.tensor.matmul(
+                        bb[:], lhsT=ones[:], rhs=brow[:, 512 * nh : 512 * (nh + 1)], start=True, stop=True
+                    )
+                    nc.scalar.copy(out=bias_bc[:, 512 * nh : 512 * (nh + 1)], in_=bb[:])
+            if c == 1:
+                after = [weave_mix(1, 0, MIX[1]), turn_syn(2), weave_mix(0, 1, MIX[2])]
+            if c == 2:
+                after = [weave_mix(1, 1, MIX[3])]
+                an_raw = []
+                for a in range(2):
+                    an_raw.append(sb([128, 2, 2048], BF16, "r8", 2))
+                    nc.sync.dma_start(out=an_raw[a][:], in_=an_v[a])
+                fre = sb([128, 2, 1024], BF16, "r4", 2)
+                nc.sync.dma_start(out=fre[:], in_=filt_re.rearrange("(i p) c -> p i c", p=128))
+                fim = sb([128, 2, 1024], BF16, "r4", 2)
+                nc.sync.dma_start(out=fim[:], in_=filt_im.rearrange("(i p) c -> p i c", p=128))
+            if c == 3:
+                after = [turn_syn(3), turn_an(0)]
+            if c in (4, 5, 6):
+                after = [turn_an(c - 3)]
+            if c == 7:
+                spec(1, 0, ("z", "z"), "gg")
+                local(3, 0, False)
+            quant_hp(c)
+            pending = after
+
+        for kind, *args in TAIL:
+            if kind == "lo":
+                local(3, args[0], args[1])
+            else:
+                spec(*args)

@@ -3,9 +3,10 @@ from contextlib import ExitStack
 import concourse.mybir as mybir
 from concourse.masks import make_identity
 
-NPTS, NFUN, NMODE, NCH = 2048, 512, 256, 1024
+NPTS, NFUN, NCH = 2048, 512, 1024
 FLOPS = 2 * (NPTS * NFUN * NCH + NPTS * NCH * NCH + NFUN * NPTS * NCH)
 
+P = 128
 F32 = mybir.dt.float32
 BF16 = mybir.dt.bfloat16
 U32 = mybir.dt.uint32
@@ -14,30 +15,59 @@ FP8X4 = mybir.dt.float8_e4m3fn_x4
 ACT = mybir.ActivationFunctionType
 ALU = mybir.AluOpType
 
-NCHUNK = 8
-LO_SCALAR = (1, 3, 5, 7)
-LO_STEP = ((), (), (0, 1, 2, 3), (4, 5, 6, 7), (0, 1, 2, 3), (4, 5, 6, 7), (0, 1, 2, 3, 4), (5, 6, 7))
-MIX = (False, True, False, True)
+START = (
+    "turnvec first0 quantin turnx0 gelu0 weavecoef skip0 first2 gain0 turnx2 gelu2 skip2 turnx1 first1 "
+    "copyvec turnin0 turnin1 copyin0 quantcoef first3 turnx3 gain2 copyin1 gelu1 gelu3 skip1 gain1 "
+    "gain3 skip3 "
+).split()
+EARLY = (
+    "first0 turnx0 gelu0 turnx2 quanthp skip0 turna0 turna1 first2 first1 quad0 quad1 turna3 turnin0 "
+    "skip2 gelu2 weavemix1 turnx1 copyin0 quad3 gelu1 quantin first3 turna2 skip1 weavehc gain0 "
+    "weavemix0 turnx3 quad2 turnin1 gain2 skip3 gelu3 quantmix0 quantmix1 copyin1 gain3 gain1 quanthc "
+).split()
+STEP = (
+    "turnx0 first0 local1 first3 gelu0 local0 turna0 skip0 store1 turnx3 weavehc gelu3 turnx2 turna2 "
+    "first2 skip3 local3 gelu2 store0 quad0 first1 turna3 turnx1 turnin0 quantmix0 local2 quanthp "
+    "quanthc gain0 quantin quad2 store3 gelu1 skip1 local4 copyin0 gain2 turna1 gain1 gain3 skip2 "
+    "store2 quad3 turnin1 copyin1 quad1 store4 "
+).split()
+LAST = (
+    "local0 turna0 weavehc quanthp turna3 store0 quad0 local1 quad3 local2 quantin store1 spec1 turna2 "
+    "store2 turna1 quanthc filter1 quad2 spec0 filter0 quad1 "
+).split()
 TAIL = (
-    ("lo", 1, True),
-    ("lo", 2, False),
-    ("spec", 0, 1, ("z", "a"), "gg"),
-    ("lo", 3, True),
-    ("lo", 4, False),
-    ("lo", 5, True),
-    ("spec", 1, 1, ("t", "z"), "vv"),
-    ("lo", 6, False),
-    ("lo", 7, True),
-)
+    "quanthp local7 store7 local0 store0 local6 store6 local1 spec0 store1 local4 filter0 local2 store4 "
+    "local3 store3 store2 local5 spec1 store5 filter1 "
+).split()
+
+LEAD = {
+    "first": 2, "skip": 2, "turnx": 1, "gelu": 1, "gain": 1,
+    "turna": 0, "quad": 0, "weavehc": 0, "quanthc": 0, "quanthp": -1,
+}
+
+GAIN = ("gg", "gs", "sg", "sg", "sg", "sg", "sg", "ss")
+WEAVE_HC = "vvssssss"
+LOCAL = {
+    2: "0s 1v 2v 3v", 3: "4s 5s 6v 7v", 4: "0s 1v 2v 3v", 5: "4s 5s 6v 7v",
+    6: "0v 1s 2v 3s 4v", 7: "5v 6s 7s", 8: "0s 1v 2s 3v 4s 5v 6v 7s",
+}
+MIX = {0: ((0, 0, "v"), (1, 0, "s")), 1: ((0, 1, "s"), (1, 1, "s"))}
+TURNED = {
+    -2: ("synth", 1), 0: ("synth", 2), 2: ("synth", 3),
+    3: ("analysis", 0), 4: ("analysis", 1), 5: ("analysis", 2), 6: ("analysis", 3),
+}
+SPEC = {
+    7: ((0, 0, "zz", "gg"), (1, 0, "zz", "gg")),
+    8: ((0, 1, "za", "vg"), (1, 1, "tz", "vv")),
+}
 
 
 def tile_fourier_operator_mix_f6_kernel(
     tc, synth, coef, skip, bias, gain, quad, mix, bias_mix, analysis, filt_re, filt_im,
-    out_local, out_cos, out_sin,
+    local, cosine, sine,
 ):
     nc = tc.nc
     with ExitStack() as ctx:
-        ctx.enter_context(nc.allow_non_contiguous_dma("per-channel and per-point vectors"))
         pool = ctx.enter_context(tc.tile_pool(name="sb", bufs=1))
         psum = ctx.enter_context(tc.psum_pool(name="ps", bufs=2))
         ctx.enter_context(tc.manual_schedule())
@@ -46,71 +76,117 @@ def tile_fourier_operator_mix_f6_kernel(
             return pool.tile(shape, dtype, name=tag, tag=tag, bufs=bufs, align_bytes=64)
 
         def bank(tag):
-            return psum.tile([128, 512], F32, name=tag, tag=tag, bufs=2)
+            return psum.tile([P, 512], F32, name=tag, tag=tag, bufs=2)
 
-        synth_v = synth.rearrange("(g p j) r -> g p j r", p=128, j=4)
-        coef_v = coef.rearrange("(p j) c -> p j c", j=4)
-        skip_v = skip.rearrange("(g p j) c -> g p j c", p=128, j=4)
-        mix_v = mix.rearrange("(h p j) c -> h p j c", p=128, j=4)
-        an_v = analysis.rearrange("(a b p) k -> a p b k", b=2, p=128)
-        local_v = out_local.rearrange("(g p j) c -> g p j c", p=128, j=4)
+        def words(group):
+            return group[:].rearrange("p n i -> p (n i)").bitcast(F32)
 
-        coef_q = sb([128, 2, 512], U32, "coef_q")
-        coef_s = sb([128, 2, 512], U8, "coef_s")
-        syn_q = sb([128, 4, 512], U32, "syn_q")
-        syn_s = sb([128, 4, 512], U8, "syn_s")
-        mix_q = sb([128, 2, 1024], U32, "mix_q")
-        mix_s = sb([128, 2, 1024], U8, "mix_s")
-        an_q = sb([128, 4, 512], U32, "an_q")
-        an_s = sb([128, 4, 512], U8, "an_s")
-        hp_q = sb([128, 4, 1024], U32, "hp_q")
-        hp_s = sb([128, 4, 1024], U8, "hp_s")
-        ident = sb([128, 128], F32, "ident")
-        ones = sb([128, 128], BF16, "ones")
-        brow = sb([128, 1024], BF16, "brow")
-        bias_bc = sb([128, 1024], F32, "bias_bc")
-        rows = sb([128, 512], BF16, "rows")
-        vec = sb([128, 8, 4], F32, "vec")
-        ident_b = sb([128, 128], BF16, "ident_b")
-        warm = sb([128, 1], F32, "warm")
+        def quantize(codes, scales, group):
+            nc.vector.quantize_mx(
+                out=codes.bitcast(FP8X4), scales=scales, in_=group[:].rearrange("p n i -> p (n i)")
+            )
+
+        def matmul(out, stationary, stationary_scale, moving, moving_scale, start, stop):
+            nc.tensor.matmul_mx(
+                out=out[:],
+                lhsT=stationary.bitcast(FP8X4), lhsT_scale=stationary_scale,
+                rhs=moving.bitcast(FP8X4), rhs_scale=moving_scale,
+                start=start, stop=stop,
+            )
+
+        def span(n, size=512):
+            return slice(size * n, size * (n + 1))
+
+        synth_v = synth.rearrange("(g p j) r -> g p j r", p=P, j=4)
+        coef_v = coef.rearrange("(p i) c -> p i c", i=4)
+        skip_v = skip.rearrange("(g p j) c -> g p j c", p=P, j=4)
+        mix_v = mix.rearrange("(r p i) c -> r p i c", p=P, i=4)
+        analysis_v = analysis.rearrange("(a b p) k -> a p b k", b=2, p=P)
+        local_v = local.rearrange("(g p j) c -> g p j c", p=P, j=4)
+
+        coef_q = sb([P, 2, 512], U32, "coef_q")
+        coef_s = sb([P, 2, 512], U8, "coef_s")
+        synth_q = sb([P, 4, 512], U32, "synth_q")
+        synth_s = sb([P, 4, 512], U8, "synth_s")
+        mix_q = sb([P, 2, 1024], U32, "mix_q")
+        mix_s = sb([P, 2, 1024], U8, "mix_s")
+        analysis_q = sb([P, 4, 512], U32, "analysis_q")
+        analysis_s = sb([P, 4, 512], U8, "analysis_s")
+        hp_q = sb([P, 4, 1024], U32, "hp_q")
+        hp_s = sb([P, 4, 1024], U8, "hp_s")
+
+        ident = sb([P, P], F32, "ident")
+        ones = sb([P, P], BF16, "ones")
+        bias_mix_row = sb([P, 1024], BF16, "bias_mix_row")
+        bias_mix_all = sb([P, 1024], F32, "bias_mix_all")
+        rows = sb([P, 512], BF16, "rows")
+        vec = sb([P, 8, 4], F32, "vec")
+        ident_b = sb([P, P], BF16, "ident_b")
+        warm = sb([P, 1], F32, "warm")
 
         nc.vector.memset(rows[:], 0.0)
         nc.vector.memset(ones[:], 1.0)
-        nc.vector.memset(brow[:], 0.0)
+        nc.vector.memset(bias_mix_row[:], 0.0)
         make_identity(nc, ident[:])
         nc.vector.tensor_copy(out=ident_b[:], in_=ident[:])
         nc.scalar.dma_start(out=rows[0:2, :], in_=bias.rearrange("(h k) -> h k", k=512))
         nc.scalar.dma_start(out=rows[2:4, :], in_=gain.rearrange("(h k) -> h k", k=512))
         nc.scalar.dma_start(out=rows[4:8, :], in_=quad.rearrange("(g k) -> g k", k=512))
-        nc.scalar.dma_start(out=brow[0:1, :], in_=bias_mix.unsqueeze(0))
+        nc.scalar.dma_start(out=bias_mix_row[0:1, :], in_=bias_mix.unsqueeze(0))
         nc.scalar.activation(out=warm[:], in_=ones[:, 0:1], func=ACT.Gelu_apprx_tanh)
 
-        syn_raw = {}
+        synth_raw = {}
         skip_raw = {}
 
-        def load_syn(g):
-            syn_raw[g] = sb([128, 4, 512], BF16, "syn_raw", 2)
-            nc.sync.dma_start(out=syn_raw[g][:], in_=synth_v[g])
+        def load_synth(g):
+            synth_raw[g] = sb([P, 4, 512], BF16, "synth_raw", 2)
+            nc.sync.dma_start(out=synth_raw[g][:], in_=synth_v[g])
 
-        def load_skip(g):
-            skip_raw[g] = sb([128, 4, 1024], BF16, "skip_raw", 2)
-            nc.sync.dma_start(out=skip_raw[g][:], in_=skip_v[g])
+        def load_skip(c):
+            skip_raw[c] = sb([P, 4, 512], BF16, "skip_raw", 4)
+            nc.sync.dma_start(out=skip_raw[c][:], in_=skip_v[c // 2][:, :, span(c % 2)])
 
-        load_syn(0)
         coef_raw = []
-        coef_raw.append(sb([128, 4, 512], BF16, "r4", 2))
-        nc.sync.dma_start(out=coef_raw[0][:], in_=coef_v[:, :, 0:512])
-        skip_raw[0] = sb([128, 4, 1024], BF16, "skip_raw", 2)
-        nc.sync.dma_start(out=skip_raw[0][:, :, 0:512], in_=skip_v[0][:, :, 0:512])
-        coef_raw.append(sb([128, 4, 512], BF16, "r4", 2))
-        nc.sync.dma_start(out=coef_raw[1][:], in_=coef_v[:, :, 512:1024])
-        nc.sync.dma_start(out=skip_raw[0][:, :, 512:1024], in_=skip_v[0][:, :, 512:1024])
-        load_syn(1)
+
+        def load_coef(h):
+            coef_raw.append(sb([P, 4, 512], BF16, "half_rows", 2))
+            nc.sync.dma_start(out=coef_raw[h][:], in_=coef_v[:, :, span(h)])
+
+        load_coef(0)
+        synth_raw[0] = sb([P, 4, 512], BF16, "synth_raw", 2)
+        for q in range(2):
+            nc.sync.dma_start(out=synth_raw[0][:, span(q, 2), :], in_=synth_v[0][:, span(q, 2), :])
+        load_skip(0)
+        load_coef(1)
         load_skip(1)
+        load_synth(1)
+        load_skip(2)
+        load_skip(3)
         mix_raw = []
-        for h in range(2):
-            mix_raw.append(sb([128, 4, 1024], BF16, "r8", 2))
-            nc.sync.dma_start(out=mix_raw[h][:], in_=mix_v[h])
+        for r in range(2):
+            mix_raw.append(sb([P, 4, 1024], BF16, "long_rows", 2))
+            nc.sync.dma_start(out=mix_raw[r][:], in_=mix_v[r])
+
+        analysis_raw = []
+        filt = []
+
+        def load_late_inputs():
+            for a in range(2):
+                analysis_raw.append(sb([P, 2, 2048], BF16, "long_rows", 2))
+                nc.sync.dma_start(out=analysis_raw[a][:], in_=analysis_v[a])
+            for f in (filt_re, filt_im):
+                filt.append(sb([P, 2, 1024], BF16, "half_rows", 2))
+                nc.sync.dma_start(out=filt[-1][:], in_=f.rearrange("(i p) c -> p i c", p=P))
+
+        vec_bank = []
+
+        def turn_vectors():
+            vec_bank.append(psum.tile([P, 4, P], BF16, name="t", tag="t", bufs=2))
+            for i in range(4):
+                nc.tensor.transpose(vec_bank[0][:, i, :], rows[:, i::4], ident_b[:])
+
+        def copy_vectors():
+            nc.vector.tensor_copy(out=vec[:], in_=vec_bank[0][:, :, 0:8].rearrange("p i r -> p r i"))
 
         def bias_col(h, t):
             return vec[:, h, t : t + 1]
@@ -121,301 +197,280 @@ def tile_fourier_operator_mix_f6_kernel(
         def quad_cols(g):
             return vec[:, 4 + g, :]
 
-        def turn_vectors():
-            tb = psum.tile([128, 4, 128], BF16, name="t", tag="t", bufs=2)
-            for t in range(4):
-                nc.tensor.transpose(tb[:, t, :], rows[:, t::4], ident_b[:])
-            nc.vector.tensor_copy(out=vec[:], in_=tb[:, :, 0:8].rearrange("p t r -> p r t"))
+        def spread_bias_mix():
+            for n in range(2):
+                out = bank("l")
+                nc.tensor.matmul(out[:], lhsT=ones[:], rhs=bias_mix_row[:, span(n)], start=True, stop=True)
+                nc.scalar.copy(out=bias_mix_all[:, span(n)], in_=out[:])
 
-        def words_of(t4):
-            return t4[:].rearrange("p c j -> p (c j)").bitcast(F32)
+        coef_group = {}
 
-        def turn(src_words, col0, grp):
-            for q in range(2):
-                tb = bank("t")
-                for u in range(2):
-                    for i in range(2):
-                        src = src_words[2 * q + i]
-                        o = (2 * u + i) * 128
-                        nc.tensor.transpose(
-                            tb[:, o : o + 128], src[:, col0 + u : col0 + 256 : 2], ident[:]
-                        )
-                nc.scalar.copy(
-                    out=words_of(grp)[:, 512 * q : 512 * (q + 1)].rearrange("p (r u) -> p r u", u=2),
-                    in_=tb[:].rearrange("p (u r) -> p r u", u=2),
-                )
-
-        def quant(codes, scales, grp):
-            nc.vector.quantize_mx(
-                out=codes.bitcast(FP8X4), scales=scales, in_=grp[:].rearrange("p c j -> p (c j)")
+        def weave_coef(h, engine):
+            coef_group[h] = sb([P, 512, 4], BF16, "group", 4)
+            engine(
+                out=coef_group[h][:].rearrange("p (t m) i -> p t m i", t=4),
+                in_=coef_raw[h][:].rearrange("p i (m t) -> p t m i", t=4),
             )
 
-        def turn_syn(g):
-            grp = sb([128, 512, 4], BF16, "grp", 4)
-            turn([syn_raw[g][:, j, :].bitcast(F32) for j in range(4)], 0, grp)
-            return lambda: quant(syn_q[:, g, :], syn_s[:, g, :], grp)
+        def quantize_coef(h):
+            quantize(coef_q[:, h, :], coef_s[:, h, :], coef_group[h])
 
-        def turn_an(k):
-            grp = sb([128, 512, 4], BF16, "grp", 4)
-            turn([an_raw[a][:, b, :].bitcast(F32) for a in range(2) for b in range(2)], 256 * k, grp)
-            return lambda: quant(an_q[:, k, :], an_s[:, k, :], grp)
+        mix_group = {}
 
-        sk = {}
+        def weave_mix(r, n, engine):
+            mix_group[r, n] = sb([P, 512, 4], BF16, "group", 4)
+            (nc.scalar.copy if engine == "s" else nc.vector.tensor_copy)(
+                out=mix_group[r, n][:], in_=mix_raw[r][:, :, span(n)].rearrange("p i c -> p c i")
+            )
 
-        def turn_skip(c):
-            g, h = c // 2, c % 2
-            sk[c] = sb([128, 2, 512, 2], BF16, "sk", 2)
-            skw = sk[c][:].rearrange("p u n e -> p (u n e)").bitcast(F32)
+        def quantize_mix(r, n):
+            quantize(mix_q[:, r, span(n)], mix_s[:, r, span(n)], mix_group[r, n])
+
+        turn_bank = {}
+        turn_group = {}
+
+        def turn_input(name, g, q):
+            if name == "synth":
+                row_tiles = [synth_raw[g][:, j, :] for j in range(4)]
+                col0 = 0
+            else:
+                row_tiles = [analysis_raw[a][:, b, :] for a in range(2) for b in range(2)]
+                col0 = 256 * g
+            out = turn_bank[name, g, q] = bank("t")
             for u in range(2):
-                tb = bank("t")
-                for j in range(4):
-                    src = skip_raw[g][:, j, :].bitcast(F32)
+                for i in range(2):
                     nc.tensor.transpose(
-                        tb[:, 128 * j : 128 * (j + 1)],
-                        src[:, 256 * h + u : 256 * (h + 1) : 2],
+                        out[:, span(2 * u + i, P)],
+                        row_tiles[2 * q + i].bitcast(F32)[:, col0 + u : col0 + 256 : 2],
                         ident[:],
                     )
-                nc.scalar.copy(out=skw[:, 512 * u : 512 * (u + 1)], in_=tb[:])
+            if name == "synth" and q == 1 and g < 2:
+                load_synth(g + 2)
 
-        act_t = {}
-        pair = {}
+        def copy_input(name, g, q):
+            if q == 0:
+                turn_group[name, g] = sb([P, 512, 4], BF16, "group", 4)
+            nc.scalar.copy(
+                out=words(turn_group[name, g])[:, span(q)].rearrange("p (r u) -> p r u", u=2),
+                in_=turn_bank[name, g, q][:].rearrange("p (u r) -> p r u", u=2),
+            )
 
-        def first(c, t):
+        def quantize_input(name, g):
+            codes, scales = (synth_q, synth_s) if name == "synth" else (analysis_q, analysis_s)
+            quantize(codes[:, g, :], scales[:, g, :], turn_group[name, g])
+
+        z_bank = {}
+        x_tile = {}
+        x_bank = {}
+        act = {}
+
+        def first_product(c, j):
             g, h = c // 2, c % 2
-            if t == 0:
-                act_t[c] = sb([128, 4, 512], F32, "act", 2)
-                pair[c] = sb([128, 2, 512, 2], BF16, "pair", 2)
-            zb = bank("z")
-            nc.tensor.matmul_mx(
-                out=zb[:],
-                lhsT=coef_q[:, h, 128 * t : 128 * (t + 1)].bitcast(FP8X4),
-                lhsT_scale=coef_s[:, h, 128 * t : 128 * (t + 1)],
-                rhs=syn_q[:, g, :].bitcast(FP8X4),
-                rhs_scale=syn_s[:, g, :],
-                start=True,
-                stop=True,
-            )
-            x = sb([128, 512], F32, "x", 6)
-            nc.vector.tensor_tensor(
-                out=x[:], in0=zb[:], in1=sk[c][:, t // 2, :, t % 2], op=ALU.add
-            )
-            nc.scalar.activation(
-                out=act_t[c][:, t, :], in_=x[:], func=ACT.Gelu_apprx_tanh, bias=bias_col(h, t)
-            )
-            nc.gpsimd.tensor_scalar(
-                out=pair[c][:, t // 2, :, t % 2],
-                in0=act_t[c][:, t, :],
-                scalar1=gain_col(h, t),
-                scalar2=0.0,
-                op0=ALU.mult,
-                op1=ALU.add,
+            z_bank[c, j] = bank("z")
+            matmul(
+                z_bank[c, j], synth_q[:, g, span(j, P)], synth_s[:, g, span(j, P)],
+                coef_q[:, h, :], coef_s[:, h, :], True, True,
             )
 
-        hc_b = {}
+        def add_skip(c, j):
+            if j == 0:
+                x_tile[c] = sb([P, 4, 512], F32, "x", 2)
+            nc.vector.tensor_tensor(
+                out=x_tile[c][:, j, :].rearrange("p (t m) -> p t m", t=4),
+                in0=z_bank[c, j][:].rearrange("p (t m) -> p t m", t=4),
+                in1=skip_raw[c][:, j, :].rearrange("p (m t) -> p t m", t=4),
+                op=ALU.add,
+            )
+            if j == 3 and c + 4 < 8:
+                load_skip(c + 4)
+
+        def turn_x(c, t):
+            x_bank[c, t] = bank("t")
+            for j in range(4):
+                nc.tensor.transpose(x_bank[c, t][:, span(j, P)], x_tile[c][:, j, span(t, P)], ident[:])
+
+        def gelu(c, t):
+            if t == 0:
+                act[c] = sb([P, 4, 512], F32, "act", 2)
+            nc.scalar.activation(
+                out=act[c][:, t, :], in_=x_bank[c, t][:], func=ACT.Gelu_apprx_tanh, bias=bias_col(c % 2, t)
+            )
+
+        hc_pair = {}
+        hc_group = {}
         hc_q = {}
         hc_s = {}
 
+        def scale_hc(c, t):
+            if t == 0:
+                hc_pair[c] = sb([P, 2, 512, 2], BF16, "hc_pair", 2)
+            out = hc_pair[c][:, t // 2, :, t % 2]
+            scale = gain_col(c % 2, t)
+            if GAIN[c][t // 2] == "g":
+                nc.gpsimd.tensor_scalar(
+                    out=out, in0=act[c][:, t, :], scalar1=scale, scalar2=0.0, op0=ALU.mult, op1=ALU.add
+                )
+            else:
+                nc.scalar.activation(out=out, in_=act[c][:, t, :], func=ACT.Copy, scale=scale)
+
         def weave_hc(c):
-            hc_b[c] = sb([128, 512, 4], BF16, "hcb", 2)
-            nc.scalar.copy(
-                out=words_of(hc_b[c]).rearrange("p (n u) -> p n u", u=2),
-                in_=pair[c][:].rearrange("p u n e -> p (u n e)").bitcast(F32).rearrange(
+            hc_group[c] = sb([P, 512, 4], BF16, "hc_group", 2)
+            (nc.scalar.copy if WEAVE_HC[c] == "s" else nc.vector.tensor_copy)(
+                out=words(hc_group[c]).rearrange("p (n u) -> p n u", u=2),
+                in_=hc_pair[c][:].rearrange("p u n e -> p (u n e)").bitcast(F32).rearrange(
                     "p (u n) -> p n u", u=2
                 ),
             )
 
-        def quant_hc(c):
+        def quantize_hc(c):
             g, h = c // 2, c % 2
             if h == 0:
-                hc_q[g] = sb([128, 2, 512], U32, "hc_q", 2)
-                hc_s[g] = sb([128, 2, 512], U8, "hc_s", 2)
-            quant(hc_q[g][:, h, :], hc_s[g][:, h, :], hc_b[c])
+                hc_q[g] = sb([P, 2, 512], U32, "hc_q", 2)
+                hc_s[g] = sb([P, 2, 512], U8, "hc_s", 2)
+            quantize(hc_q[g][:, h, :], hc_s[g][:, h, :], hc_group[c])
 
-        hp_b = {}
+        a_bank = {}
+        hp_group = {}
 
         def turn_act(c, t):
-            g = c // 2
-            if t == 0:
-                hp_b[c] = sb([128, 512, 4], BF16, "hpb", 2)
-            tb = bank("a")
+            a_bank[c, t] = bank("a")
             for j in range(4):
-                nc.tensor.transpose(
-                    tb[:, 128 * j : 128 * (j + 1)],
-                    act_t[c][:, t, 128 * j : 128 * (j + 1)],
-                    ident[:],
-                )
+                nc.tensor.transpose(a_bank[c, t][:, span(j, P)], act[c][:, t, span(j, P)], ident[:])
+
+        def scale_hp(c, t):
+            if t == 0:
+                hp_group[c] = sb([P, 512, 4], BF16, "hp_group", 2)
             nc.vector.tensor_tensor(
-                out=hp_b[c][:, 128 * t : 128 * (t + 1), :],
-                in0=tb[:].rearrange("p (j m) -> p m j", j=4),
-                in1=quad_cols(g).unsqueeze(1).to_broadcast([128, 128, 4]),
+                out=hp_group[c][:, span(t, P), :],
+                in0=a_bank[c, t][:].rearrange("p (j m) -> p m j", j=4),
+                in1=quad_cols(c // 2).unsqueeze(1).to_broadcast([P, P, 4]),
                 op=ALU.mult,
             )
 
-        def quant_hp(c):
+        def quantize_hp(c):
             g, h = c // 2, c % 2
-            cols = slice(512 * h, 512 * (h + 1))
-            quant(hp_q[:, g, cols], hp_s[:, g, cols], hp_b[c])
+            quantize(hp_q[:, g, span(h)], hp_s[:, g, span(h)], hp_group[c])
 
+        local_bank = {}
 
-        def local(g, i, on_scalar):
-            nh, j = i // 4, i % 4
-            cols = slice(512 * nh, 512 * (nh + 1))
-            lb = bank("l")
+        def local_product(g, i):
+            n, j = i // 4, i % 4
+            local_bank[g, i] = bank("l")
             for h in range(2):
-                nc.tensor.matmul_mx(
-                    out=lb[:],
-                    lhsT=hc_q[g][:, h, 128 * j : 128 * (j + 1)].bitcast(FP8X4),
-                    lhsT_scale=hc_s[g][:, h, 128 * j : 128 * (j + 1)],
-                    rhs=mix_q[:, h, cols].bitcast(FP8X4),
-                    rhs_scale=mix_s[:, h, cols],
-                    start=(h == 0),
-                    stop=(h == 1),
+                matmul(
+                    local_bank[g, i], hc_q[g][:, h, span(j, P)], hc_s[g][:, h, span(j, P)],
+                    mix_q[:, h, span(n)], mix_s[:, h, span(n)], h == 0, h == 1,
                 )
-            o = sb([128, 512], F32, "lout", 8)
-            if on_scalar:
-                nc.scalar.copy(out=o[:], in_=lb[:])
-                nc.gpsimd.tensor_tensor(out=o[:], in0=o[:], in1=bias_bc[:, cols], op=ALU.add)
+
+        def store_local(g, i, engine):
+            n, j = i // 4, i % 4
+            out = sb([P, 512], F32, "local_out", 8)
+            if engine == "s":
+                nc.scalar.copy(out=out[:], in_=local_bank[g, i][:])
+                nc.gpsimd.tensor_tensor(out=out[:], in0=out[:], in1=bias_mix_all[:, span(n)], op=ALU.add)
             else:
-                nc.vector.tensor_tensor(out=o[:], in0=lb[:], in1=bias_bc[:, cols], op=ALU.add)
-            nc.sync.dma_start(out=local_v[g][:, j, cols], in_=o[:])
-
-        coef_g = {}
-
-        def weave_coef(h):
-            coef_g[h] = sb([128, 512, 4], BF16, "grp", 4)
-            nc.vector.tensor_copy(
-                out=coef_g[h][:].rearrange("p (t m) j -> p t m j", t=4),
-                in_=coef_raw[h][:].rearrange("p j (m t) -> p t m j", t=4),
-            )
-
-        def weave_mix(h, nh, on_scalar):
-            grp = sb([128, 512, 4], BF16, "grp", 4)
-            src = mix_raw[h][:, :, 512 * nh : 512 * (nh + 1)].rearrange("p j c -> p c j")
-            if on_scalar:
-                nc.scalar.copy(out=grp[:], in_=src)
-            else:
-                nc.vector.tensor_copy(out=grp[:], in_=src)
-            cols = slice(512 * nh, 512 * (nh + 1))
-            return lambda: quant(mix_q[:, h, cols], mix_s[:, h, cols], grp)
-
-        spec_n = [0]
-
-        def spec(i, h, tags, add_engines):
-            cols = slice(512 * h, 512 * (h + 1))
-            zz = []
-            for part in range(2):
-                mt = 2 * part + i
-                sbk = bank(tags[part])
-                for g in range(4):
-                    nc.tensor.matmul_mx(
-                        out=sbk[:],
-                        lhsT=an_q[:, g, 128 * mt : 128 * (mt + 1)].bitcast(FP8X4),
-                        lhsT_scale=an_s[:, g, 128 * mt : 128 * (mt + 1)],
-                        rhs=hp_q[:, g, cols].bitcast(FP8X4),
-                        rhs_scale=hp_s[:, g, cols],
-                        start=(g == 0),
-                        stop=(g == 3),
-                    )
-                zz.append(sbk[:].rearrange("p (t m) -> p m t", t=4))
-            fr = fre[:, i, cols].rearrange("p (m t) -> p m t", t=4)
-            fi = fim[:, i, cols].rearrange("p (m t) -> p m t", t=4)
-            prods = []
-            for f, z in ((fr, zz[0]), (fi, zz[0]), (fi, zz[1]), (fr, zz[1])):
-                pt = sb([128, 512], F32, "x", 6)
                 nc.vector.tensor_tensor(
-                    out=pt[:].rearrange("p (m t) -> p m t", t=4), in0=z, in1=f, op=ALU.mult
+                    out=out[:], in0=local_bank[g, i][:], in1=bias_mix_all[:, span(n)], op=ALU.add
                 )
-                prods.append(pt)
-            for a, b, op, dst, e in (
-                (prods[0], prods[2], ALU.add, out_cos, add_engines[0]),
-                (prods[3], prods[1], ALU.subtract, out_sin, add_engines[1]),
-            ):
-                o = sb([128, 512], F32, "fo", 3)
-                eng = nc.gpsimd if e == "g" else nc.vector
-                eng.tensor_tensor(out=o[:], in0=a[:], in1=b[:], op=op)
-                nc.sync.dma_start(out=dst[128 * i : 128 * (i + 1), cols], in_=o[:])
+            nc.sync.dma_start(out=local_v[g][:, j, span(n)], in_=out[:])
 
-        q_syn0 = turn_syn(0)
-        load_syn(2)
-        weave_coef(0)
-        q_syn0()
-        quant(coef_q[:, 0, :], coef_s[:, 0, :], coef_g[0])
-        turn_skip(0)
-        turn_vectors()
-        weave_coef(1)
-        first(0, 0)
-        quant(coef_q[:, 1, :], coef_s[:, 1, :], coef_g[1])
-        first(0, 1)
-        turn_skip(1)
-        load_skip(2)
-        first(0, 2)
-        first(0, 3)
-        q_syn1 = turn_syn(1)
-        load_syn(3)
-        pending = [q_syn1]
+        spec_bank = {}
 
-        for c in range(NCHUNK):
-            los = [((c - 2) // 2, i) for i in LO_STEP[c]]
-            half = (len(los) + 1) // 2
-
-            if c + 1 < NCHUNK:
-                first(c + 1, 0)
-                first(c + 1, 1)
-            for q in pending:
-                q()
-            pending = []
-            for g, i in los[:half]:
-                local(g, i, i in LO_SCALAR)
-            turn_act(c, 0)
-            turn_act(c, 1)
-            if c + 2 < NCHUNK:
-                turn_skip(c + 2)
-                if c == 1:
-                    load_skip(3)
-            weave_hc(c)
-            if c + 1 < NCHUNK:
-                first(c + 1, 2)
-                first(c + 1, 3)
-            for g, i in los[half:]:
-                local(g, i, i in LO_SCALAR)
-            if c == 7:
-                spec(0, 0, ("z", "z"), "gg")
-            quant_hc(c)
-            turn_act(c, 2)
-            turn_act(c, 3)
-            after = []
-            if c == 0:
-                after = [weave_mix(0, 0, MIX[0])]
-                for nh in range(2):
-                    bb = bank("l")
-                    nc.tensor.matmul(
-                        bb[:], lhsT=ones[:], rhs=brow[:, 512 * nh : 512 * (nh + 1)], start=True, stop=True
+        def spec_product(i, h, tags):
+            for part in range(2):
+                rows_of_spec = span(2 * part + i, P)
+                spec_bank[i, h, part] = bank(tags[part])
+                for g in range(4):
+                    matmul(
+                        spec_bank[i, h, part],
+                        analysis_q[:, g, rows_of_spec], analysis_s[:, g, rows_of_spec],
+                        hp_q[:, g, span(h)], hp_s[:, g, span(h)], g == 0, g == 3,
                     )
-                    nc.scalar.copy(out=bias_bc[:, 512 * nh : 512 * (nh + 1)], in_=bb[:])
-            if c == 1:
-                after = [weave_mix(1, 0, MIX[1]), turn_syn(2), weave_mix(0, 1, MIX[2])]
-            if c == 2:
-                after = [weave_mix(1, 1, MIX[3])]
-                an_raw = []
-                for a in range(2):
-                    an_raw.append(sb([128, 2, 2048], BF16, "r8", 2))
-                    nc.sync.dma_start(out=an_raw[a][:], in_=an_v[a])
-                fre = sb([128, 2, 1024], BF16, "r4", 2)
-                nc.sync.dma_start(out=fre[:], in_=filt_re.rearrange("(i p) c -> p i c", p=128))
-                fim = sb([128, 2, 1024], BF16, "r4", 2)
-                nc.sync.dma_start(out=fim[:], in_=filt_im.rearrange("(i p) c -> p i c", p=128))
-            if c == 3:
-                after = [turn_syn(3), turn_an(0)]
-            if c in (4, 5, 6):
-                after = [turn_an(c - 3)]
-            if c == 7:
-                spec(1, 0, ("z", "z"), "gg")
-                local(3, 0, False)
-            quant_hp(c)
-            pending = after
 
-        for kind, *args in TAIL:
-            if kind == "lo":
-                local(3, args[0], args[1])
-            else:
-                spec(*args)
+        def apply_filter(i, h, engines):
+            zc, zs = [spec_bank[i, h, part][:].rearrange("p (t m) -> p m t", t=4) for part in range(2)]
+            fr, fi = [f[:, i, span(h)].rearrange("p (m t) -> p m t", t=4) for f in filt]
+            products = []
+            for f, z in ((fr, zc), (fi, zc), (fi, zs), (fr, zs)):
+                product = sb([P, 512], F32, "product", 6)
+                nc.vector.tensor_tensor(
+                    out=product[:].rearrange("p (m t) -> p m t", t=4), in0=z, in1=f, op=ALU.mult
+                )
+                products.append(product)
+            fr_zc, fi_zc, fi_zs, fr_zs = products
+            for x, y, op, dst, engine in (
+                (fr_zc, fi_zs, ALU.add, cosine, engines[0]),
+                (fr_zs, fi_zc, ALU.subtract, sine, engines[1]),
+            ):
+                out = sb([P, 512], F32, "filter_out", 3)
+                (nc.gpsimd if engine == "g" else nc.vector).tensor_tensor(out=out[:], in0=x[:], in1=y[:], op=op)
+                nc.sync.dma_start(out=dst[span(i, P), span(h)], in_=out[:])
+
+        chunk_ops = {
+            "first": first_product, "skip": add_skip, "turnx": turn_x, "gelu": gelu, "gain": scale_hc,
+            "turna": turn_act, "quad": scale_hp,
+            "weavehc": lambda c, k: weave_hc(c),
+            "quanthc": lambda c, k: quantize_hc(c),
+            "quanthp": lambda c, k: quantize_hp(c),
+        }
+
+        def run(entry, step):
+            numbered = entry[-1] in "01234567"
+            name = entry[:-1] if numbered else entry
+            part = int(entry[-1]) if numbered else 0
+            if name in LEAD:
+                c = step + LEAD[name]
+                if 0 <= c < 8:
+                    chunk_ops[name](c, part)
+            elif name in ("local", "store"):
+                items = LOCAL.get(step, "").split()
+                if part < len(items):
+                    g, i, engine = (step - 2) // 2, int(items[part][0]), items[part][1]
+                    if name == "local":
+                        local_product(g, i)
+                    else:
+                        store_local(g, i, engine)
+            elif name in ("turnin", "copyin"):
+                if step in TURNED:
+                    (turn_input if name == "turnin" else copy_input)(*TURNED[step], part)
+            elif name == "quantin":
+                if step - 1 in TURNED:
+                    quantize_input(*TURNED[step - 1])
+            elif name == "weavemix":
+                if step in MIX:
+                    weave_mix(*MIX[step][part])
+            elif name == "quantmix":
+                s = step - 1 if part == 0 else step
+                if s in MIX:
+                    quantize_mix(*MIX[s][part][0:2])
+            elif name in ("spec", "filter"):
+                i, h, tags, engines = SPEC[step][part]
+                if name == "spec":
+                    spec_product(i, h, tags)
+                else:
+                    apply_filter(i, h, engines)
+            elif step == -2:
+                if name == "turnvec":
+                    turn_vectors()
+                elif name == "copyvec":
+                    copy_vectors()
+                elif name == "weavecoef":
+                    weave_coef(1, nc.scalar.copy)
+                else:
+                    quantize_coef(1)
+
+        weave_coef(0, nc.vector.tensor_copy)
+        for q in range(2):
+            turn_input("synth", 0, q)
+            copy_input("synth", 0, q)
+        quantize_coef(0)
+        quantize_input("synth", 0)
+
+        for step in range(-2, 9):
+            if step == 1:
+                spread_bias_mix()
+            if step == 3:
+                load_late_inputs()
+            order = START if step < 0 else EARLY if step < 2 else STEP if step < 7 else LAST if step < 8 else TAIL
+            for entry in order:
+                run(entry, step)

from contextlib import ExitStack

import concourse.mybir as mybir
from concourse.masks import make_identity

NPTS, NFUN, NCH = 2048, 512, 1024
FLOPS = 2 * (NPTS * NFUN * NCH + NPTS * NCH * NCH + NFUN * NPTS * NCH)

P = 128
F32 = mybir.dt.float32
BF16 = mybir.dt.bfloat16
U32 = mybir.dt.uint32
U8 = mybir.dt.uint8
FP8X4 = mybir.dt.float8_e4m3fn_x4
ACT = mybir.ActivationFunctionType
ALU = mybir.AluOpType

START = (
    "turnvec first0 quantin turnx0 gelu0 weavecoef skip0 first2 gain0 turnx2 gelu2 skip2 turnx1 first1 "
    "copyvec turnin0 turnin1 copyin0 quantcoef first3 turnx3 gain2 copyin1 gelu1 gelu3 skip1 gain1 "
    "gain3 skip3 "
).split()
EARLY = (
    "first0 turnx0 gelu0 turnx2 quanthp skip0 turna0 turna1 first2 first1 quad0 quad1 turna3 turnin0 "
    "skip2 gelu2 weavemix1 turnx1 copyin0 quad3 gelu1 quantin first3 turna2 skip1 weavehc gain0 "
    "weavemix0 turnx3 quad2 turnin1 gain2 skip3 gelu3 quantmix0 quantmix1 copyin1 gain3 gain1 quanthc "
).split()
STEP = (
    "turnx0 first0 local1 first3 gelu0 local0 turna0 skip0 store1 turnx3 weavehc gelu3 turnx2 turna2 "
    "first2 skip3 local3 gelu2 store0 quad0 first1 turna3 turnx1 turnin0 quantmix0 local2 quanthp "
    "quanthc gain0 quantin quad2 store3 gelu1 skip1 local4 copyin0 gain2 turna1 gain1 gain3 skip2 "
    "store2 quad3 turnin1 copyin1 quad1 store4 "
).split()
LAST = (
    "local0 turna0 weavehc quanthp turna3 store0 quad0 local1 quad3 local2 quantin store1 spec1 turna2 "
    "store2 turna1 quanthc filter1 quad2 spec0 filter0 quad1 "
).split()
TAIL = (
    "quanthp local7 store7 local0 store0 local6 store6 local1 spec0 store1 local4 filter0 local2 store4 "
    "local3 store3 store2 local5 spec1 store5 filter1 "
).split()

LEAD = {
    "first": 2, "skip": 2, "turnx": 1, "gelu": 1, "gain": 1,
    "turna": 0, "quad": 0, "weavehc": 0, "quanthc": 0, "quanthp": -1,
}

GAIN = ("gg", "gs", "sg", "sg", "sg", "sg", "sg", "ss")
WEAVE_HC = "vvssssss"
LOCAL = {
    2: "0s 1v 2v 3v", 3: "4s 5s 6v 7v", 4: "0s 1v 2v 3v", 5: "4s 5s 6v 7v",
    6: "0v 1s 2v 3s 4v", 7: "5v 6s 7s", 8: "0s 1v 2s 3v 4s 5v 6v 7s",
}
MIX = {0: ((0, 0, "v"), (1, 0, "s")), 1: ((0, 1, "s"), (1, 1, "s"))}
TURNED = {
    -2: ("synth", 1), 0: ("synth", 2), 2: ("synth", 3),
    3: ("analysis", 0), 4: ("analysis", 1), 5: ("analysis", 2), 6: ("analysis", 3),
}
SPEC = {
    7: ((0, 0, "zz", "gg"), (1, 0, "zz", "gg")),
    8: ((0, 1, "za", "vg"), (1, 1, "tz", "vv")),
}


def tile_fourier_operator_mix_f6_kernel(
    tc, synth, coef, skip, bias, gain, quad, mix, bias_mix, analysis, filt_re, filt_im,
    local, cosine, sine,
):
    nc = tc.nc
    with ExitStack() as ctx:
        pool = ctx.enter_context(tc.tile_pool(name="sb", bufs=1))
        psum = ctx.enter_context(tc.psum_pool(name="ps", bufs=2))
        ctx.enter_context(tc.manual_schedule())

        def sb(shape, dtype, tag, bufs=1):
            return pool.tile(shape, dtype, name=tag, tag=tag, bufs=bufs, align_bytes=64)

        def bank(tag):
            return psum.tile([P, 512], F32, name=tag, tag=tag, bufs=2)

        def words(group):
            return group[:].rearrange("p n i -> p (n i)").bitcast(F32)

        def quantize(codes, scales, group):
            nc.vector.quantize_mx(
                out=codes.bitcast(FP8X4), scales=scales, in_=group[:].rearrange("p n i -> p (n i)")
            )

        def matmul(out, stationary, stationary_scale, moving, moving_scale, start, stop):
            nc.tensor.matmul_mx(
                out=out[:],
                lhsT=stationary.bitcast(FP8X4), lhsT_scale=stationary_scale,
                rhs=moving.bitcast(FP8X4), rhs_scale=moving_scale,
                start=start, stop=stop,
            )

        def span(n, size=512):
            return slice(size * n, size * (n + 1))

        synth_v = synth.rearrange("(g p j) r -> g p j r", p=P, j=4)
        coef_v = coef.rearrange("(p i) c -> p i c", i=4)
        skip_v = skip.rearrange("(g p j) c -> g p j c", p=P, j=4)
        mix_v = mix.rearrange("(r p i) c -> r p i c", p=P, i=4)
        analysis_v = analysis.rearrange("(a b p) k -> a p b k", b=2, p=P)
        local_v = local.rearrange("(g p j) c -> g p j c", p=P, j=4)

        coef_q = sb([P, 2, 512], U32, "coef_q")
        coef_s = sb([P, 2, 512], U8, "coef_s")
        synth_q = sb([P, 4, 512], U32, "synth_q")
        synth_s = sb([P, 4, 512], U8, "synth_s")
        mix_q = sb([P, 2, 1024], U32, "mix_q")
        mix_s = sb([P, 2, 1024], U8, "mix_s")
        analysis_q = sb([P, 4, 512], U32, "analysis_q")
        analysis_s = sb([P, 4, 512], U8, "analysis_s")
        hp_q = sb([P, 4, 1024], U32, "hp_q")
        hp_s = sb([P, 4, 1024], U8, "hp_s")

        ident = sb([P, P], F32, "ident")
        ones = sb([P, P], BF16, "ones")
        bias_mix_row = sb([P, 1024], BF16, "bias_mix_row")
        bias_mix_all = sb([P, 1024], F32, "bias_mix_all")
        rows = sb([P, 512], BF16, "rows")
        vec = sb([P, 8, 4], F32, "vec")
        ident_b = sb([P, P], BF16, "ident_b")
        warm = sb([P, 1], F32, "warm")

        nc.vector.memset(rows[:], 0.0)
        nc.vector.memset(ones[:], 1.0)
        nc.vector.memset(bias_mix_row[:], 0.0)
        make_identity(nc, ident[:])
        nc.vector.tensor_copy(out=ident_b[:], in_=ident[:])
        nc.scalar.dma_start(out=rows[0:2, :], in_=bias.rearrange("(h k) -> h k", k=512))
        nc.scalar.dma_start(out=rows[2:4, :], in_=gain.rearrange("(h k) -> h k", k=512))
        nc.scalar.dma_start(out=rows[4:8, :], in_=quad.rearrange("(g k) -> g k", k=512))
        nc.scalar.dma_start(out=bias_mix_row[0:1, :], in_=bias_mix.unsqueeze(0))
        nc.scalar.activation(out=warm[:], in_=ones[:, 0:1], func=ACT.Gelu_apprx_tanh)

        synth_raw = {}
        skip_raw = {}

        def load_synth(g):
            synth_raw[g] = sb([P, 4, 512], BF16, "synth_raw", 2)
            nc.sync.dma_start(out=synth_raw[g][:], in_=synth_v[g])

        def load_skip(c):
            skip_raw[c] = sb([P, 4, 512], BF16, "skip_raw", 4)
            nc.sync.dma_start(out=skip_raw[c][:], in_=skip_v[c // 2][:, :, span(c % 2)])

        coef_raw = []

        def load_coef(h):
            coef_raw.append(sb([P, 4, 512], BF16, "half_rows", 2))
            nc.sync.dma_start(out=coef_raw[h][:], in_=coef_v[:, :, span(h)])

        load_coef(0)
        synth_raw[0] = sb([P, 4, 512], BF16, "synth_raw", 2)
        for q in range(2):
            nc.sync.dma_start(out=synth_raw[0][:, span(q, 2), :], in_=synth_v[0][:, span(q, 2), :])
        load_skip(0)
        load_coef(1)
        load_skip(1)
        load_synth(1)
        load_skip(2)
        load_skip(3)
        mix_raw = []
        for r in range(2):
            mix_raw.append(sb([P, 4, 1024], BF16, "long_rows", 2))
            nc.sync.dma_start(out=mix_raw[r][:], in_=mix_v[r])

        analysis_raw = []
        filt = []

        def load_late_inputs():
            for a in range(2):
                analysis_raw.append(sb([P, 2, 2048], BF16, "long_rows", 2))
                nc.sync.dma_start(out=analysis_raw[a][:], in_=analysis_v[a])
            for f in (filt_re, filt_im):
                filt.append(sb([P, 2, 1024], BF16, "half_rows", 2))
                nc.sync.dma_start(out=filt[-1][:], in_=f.rearrange("(i p) c -> p i c", p=P))

        vec_bank = []

        def turn_vectors():
            vec_bank.append(psum.tile([P, 4, P], BF16, name="t", tag="t", bufs=2))
            for i in range(4):
                nc.tensor.transpose(vec_bank[0][:, i, :], rows[:, i::4], ident_b[:])

        def copy_vectors():
            nc.vector.tensor_copy(out=vec[:], in_=vec_bank[0][:, :, 0:8].rearrange("p i r -> p r i"))

        def bias_col(h, t):
            return vec[:, h, t : t + 1]

        def gain_col(h, t):
            return vec[:, 2 + h, t : t + 1]

        def quad_cols(g):
            return vec[:, 4 + g, :]

        def spread_bias_mix():
            for n in range(2):
                out = bank("l")
                nc.tensor.matmul(out[:], lhsT=ones[:], rhs=bias_mix_row[:, span(n)], start=True, stop=True)
                nc.scalar.copy(out=bias_mix_all[:, span(n)], in_=out[:])

        coef_group = {}

        def weave_coef(h, engine):
            coef_group[h] = sb([P, 512, 4], BF16, "group", 4)
            engine(
                out=coef_group[h][:].rearrange("p (t m) i -> p t m i", t=4),
                in_=coef_raw[h][:].rearrange("p i (m t) -> p t m i", t=4),
            )

        def quantize_coef(h):
            quantize(coef_q[:, h, :], coef_s[:, h, :], coef_group[h])

        mix_group = {}

        def weave_mix(r, n, engine):
            mix_group[r, n] = sb([P, 512, 4], BF16, "group", 4)
            (nc.scalar.copy if engine == "s" else nc.vector.tensor_copy)(
                out=mix_group[r, n][:], in_=mix_raw[r][:, :, span(n)].rearrange("p i c -> p c i")
            )

        def quantize_mix(r, n):
            quantize(mix_q[:, r, span(n)], mix_s[:, r, span(n)], mix_group[r, n])

        turn_bank = {}
        turn_group = {}

        def turn_input(name, g, q):
            if name == "synth":
                row_tiles = [synth_raw[g][:, j, :] for j in range(4)]
                col0 = 0
            else:
                row_tiles = [analysis_raw[a][:, b, :] for a in range(2) for b in range(2)]
                col0 = 256 * g
            out = turn_bank[name, g, q] = bank("t")
            for u in range(2):
                for i in range(2):
                    nc.tensor.transpose(
                        out[:, span(2 * u + i, P)],
                        row_tiles[2 * q + i].bitcast(F32)[:, col0 + u : col0 + 256 : 2],
                        ident[:],
                    )
            if name == "synth" and q == 1 and g < 2:
                load_synth(g + 2)

        def copy_input(name, g, q):
            if q == 0:
                turn_group[name, g] = sb([P, 512, 4], BF16, "group", 4)
            nc.scalar.copy(
                out=words(turn_group[name, g])[:, span(q)].rearrange("p (r u) -> p r u", u=2),
                in_=turn_bank[name, g, q][:].rearrange("p (u r) -> p r u", u=2),
            )

        def quantize_input(name, g):
            codes, scales = (synth_q, synth_s) if name == "synth" else (analysis_q, analysis_s)
            quantize(codes[:, g, :], scales[:, g, :], turn_group[name, g])

        z_bank = {}
        x_tile = {}
        x_bank = {}
        act = {}

        def first_product(c, j):
            g, h = c // 2, c % 2
            z_bank[c, j] = bank("z")
            matmul(
                z_bank[c, j], synth_q[:, g, span(j, P)], synth_s[:, g, span(j, P)],
                coef_q[:, h, :], coef_s[:, h, :], True, True,
            )

        def add_skip(c, j):
            if j == 0:
                x_tile[c] = sb([P, 4, 512], F32, "x", 2)
            nc.vector.tensor_tensor(
                out=x_tile[c][:, j, :].rearrange("p (t m) -> p t m", t=4),
                in0=z_bank[c, j][:].rearrange("p (t m) -> p t m", t=4),
                in1=skip_raw[c][:, j, :].rearrange("p (m t) -> p t m", t=4),
                op=ALU.add,
            )
            if j == 3 and c + 4 < 8:
                load_skip(c + 4)

        def turn_x(c, t):
            x_bank[c, t] = bank("t")
            for j in range(4):
                nc.tensor.transpose(x_bank[c, t][:, span(j, P)], x_tile[c][:, j, span(t, P)], ident[:])

        def gelu(c, t):
            if t == 0:
                act[c] = sb([P, 4, 512], F32, "act", 2)
            nc.scalar.activation(
                out=act[c][:, t, :], in_=x_bank[c, t][:], func=ACT.Gelu_apprx_tanh, bias=bias_col(c % 2, t)
            )

        hc_pair = {}
        hc_group = {}
        hc_q = {}
        hc_s = {}

        def scale_hc(c, t):
            if t == 0:
                hc_pair[c] = sb([P, 2, 512, 2], BF16, "hc_pair", 2)
            out = hc_pair[c][:, t // 2, :, t % 2]
            scale = gain_col(c % 2, t)
            if GAIN[c][t // 2] == "g":
                nc.gpsimd.tensor_scalar(
                    out=out, in0=act[c][:, t, :], scalar1=scale, scalar2=0.0, op0=ALU.mult, op1=ALU.add
                )
            else:
                nc.scalar.activation(out=out, in_=act[c][:, t, :], func=ACT.Copy, scale=scale)

        def weave_hc(c):
            hc_group[c] = sb([P, 512, 4], BF16, "hc_group", 2)
            (nc.scalar.copy if WEAVE_HC[c] == "s" else nc.vector.tensor_copy)(
                out=words(hc_group[c]).rearrange("p (n u) -> p n u", u=2),
                in_=hc_pair[c][:].rearrange("p u n e -> p (u n e)").bitcast(F32).rearrange(
                    "p (u n) -> p n u", u=2
                ),
            )

        def quantize_hc(c):
            g, h = c // 2, c % 2
            if h == 0:
                hc_q[g] = sb([P, 2, 512], U32, "hc_q", 2)
                hc_s[g] = sb([P, 2, 512], U8, "hc_s", 2)
            quantize(hc_q[g][:, h, :], hc_s[g][:, h, :], hc_group[c])

        a_bank = {}
        hp_group = {}

        def turn_act(c, t):
            a_bank[c, t] = bank("a")
            for j in range(4):
                nc.tensor.transpose(a_bank[c, t][:, span(j, P)], act[c][:, t, span(j, P)], ident[:])

        def scale_hp(c, t):
            if t == 0:
                hp_group[c] = sb([P, 512, 4], BF16, "hp_group", 2)
            nc.vector.tensor_tensor(
                out=hp_group[c][:, span(t, P), :],
                in0=a_bank[c, t][:].rearrange("p (j m) -> p m j", j=4),
                in1=quad_cols(c // 2).unsqueeze(1).to_broadcast([P, P, 4]),
                op=ALU.mult,
            )

        def quantize_hp(c):
            g, h = c // 2, c % 2
            quantize(hp_q[:, g, span(h)], hp_s[:, g, span(h)], hp_group[c])

        local_bank = {}

        def local_product(g, i):
            n, j = i // 4, i % 4
            local_bank[g, i] = bank("l")
            for h in range(2):
                matmul(
                    local_bank[g, i], hc_q[g][:, h, span(j, P)], hc_s[g][:, h, span(j, P)],
                    mix_q[:, h, span(n)], mix_s[:, h, span(n)], h == 0, h == 1,
                )

        def store_local(g, i, engine):
            n, j = i // 4, i % 4
            out = sb([P, 512], F32, "local_out", 8)
            if engine == "s":
                nc.scalar.copy(out=out[:], in_=local_bank[g, i][:])
                nc.gpsimd.tensor_tensor(out=out[:], in0=out[:], in1=bias_mix_all[:, span(n)], op=ALU.add)
            else:
                nc.vector.tensor_tensor(
                    out=out[:], in0=local_bank[g, i][:], in1=bias_mix_all[:, span(n)], op=ALU.add
                )
            nc.sync.dma_start(out=local_v[g][:, j, span(n)], in_=out[:])

        spec_bank = {}

        def spec_product(i, h, tags):
            for part in range(2):
                rows_of_spec = span(2 * part + i, P)
                spec_bank[i, h, part] = bank(tags[part])
                for g in range(4):
                    matmul(
                        spec_bank[i, h, part],
                        analysis_q[:, g, rows_of_spec], analysis_s[:, g, rows_of_spec],
                        hp_q[:, g, span(h)], hp_s[:, g, span(h)], g == 0, g == 3,
                    )

        def apply_filter(i, h, engines):
            zc, zs = [spec_bank[i, h, part][:].rearrange("p (t m) -> p m t", t=4) for part in range(2)]
            fr, fi = [f[:, i, span(h)].rearrange("p (m t) -> p m t", t=4) for f in filt]
            products = []
            for f, z in ((fr, zc), (fi, zc), (fi, zs), (fr, zs)):
                product = sb([P, 512], F32, "product", 6)
                nc.vector.tensor_tensor(
                    out=product[:].rearrange("p (m t) -> p m t", t=4), in0=z, in1=f, op=ALU.mult
                )
                products.append(product)
            fr_zc, fi_zc, fi_zs, fr_zs = products
            for x, y, op, dst, engine in (
                (fr_zc, fi_zs, ALU.add, cosine, engines[0]),
                (fr_zs, fi_zc, ALU.subtract, sine, engines[1]),
            ):
                out = sb([P, 512], F32, "filter_out", 3)
                (nc.gpsimd if engine == "g" else nc.vector).tensor_tensor(out=out[:], in0=x[:], in1=y[:], op=op)
                nc.sync.dma_start(out=dst[span(i, P), span(h)], in_=out[:])

        chunk_ops = {
            "first": first_product, "skip": add_skip, "turnx": turn_x, "gelu": gelu, "gain": scale_hc,
            "turna": turn_act, "quad": scale_hp,
            "weavehc": lambda c, k: weave_hc(c),
            "quanthc": lambda c, k: quantize_hc(c),
            "quanthp": lambda c, k: quantize_hp(c),
        }

        def run(entry, step):
            numbered = entry[-1] in "01234567"
            name = entry[:-1] if numbered else entry
            part = int(entry[-1]) if numbered else 0
            if name in LEAD:
                c = step + LEAD[name]
                if 0 <= c < 8:
                    chunk_ops[name](c, part)
            elif name in ("local", "store"):
                items = LOCAL.get(step, "").split()
                if part < len(items):
                    g, i, engine = (step - 2) // 2, int(items[part][0]), items[part][1]
                    if name == "local":
                        local_product(g, i)
                    else:
                        store_local(g, i, engine)
            elif name in ("turnin", "copyin"):
                if step in TURNED:
                    (turn_input if name == "turnin" else copy_input)(*TURNED[step], part)
            elif name == "quantin":
                if step - 1 in TURNED:
                    quantize_input(*TURNED[step - 1])
            elif name == "weavemix":
                if step in MIX:
                    weave_mix(*MIX[step][part])
            elif name == "quantmix":
                s = step - 1 if part == 0 else step
                if s in MIX:
                    quantize_mix(*MIX[s][part][0:2])
            elif name in ("spec", "filter"):
                i, h, tags, engines = SPEC[step][part]
                if name == "spec":
                    spec_product(i, h, tags)
                else:
                    apply_filter(i, h, engines)
            elif step == -2:
                if name == "turnvec":
                    turn_vectors()
                elif name == "copyvec":
                    copy_vectors()
                elif name == "weavecoef":
                    weave_coef(1, nc.scalar.copy)
                else:
                    quantize_coef(1)

        weave_coef(0, nc.vector.tensor_copy)
        for q in range(2):
            turn_input("synth", 0, q)
            copy_input("synth", 0, q)
        quantize_coef(0)
        quantize_input("synth", 0)

        for step in range(-2, 9):
            if step == 1:
                spread_bias_mix()
            if step == 3:
                load_late_inputs()
            order = START if step < 0 else EARLY if step < 2 else STEP if step < 7 else LAST if step < 8 else TAIL
            for entry in order:
                run(entry, step)
